import numpy as np
import ml_dtypes


def mxq(x, axis, fmt="e4m3"):
    dtype, down = {"e4m3": (ml_dtypes.float8_e4m3fn, 7), "e5m2": (ml_dtypes.float8_e5m2, 14)}[fmt]
    v = np.moveaxis(np.asarray(x, np.float32).astype(ml_dtypes.bfloat16).astype(np.float64), axis, -1)
    blocks = v.reshape(v.shape[:-1] + (-1, 32))
    amax = np.abs(blocks).max(-1, keepdims=True)
    byte = np.maximum(np.where(amax > 0, np.frexp(amax)[1] - 1 + 127, 0) - down, 1)
    scale = np.exp2(byte - 127.0)
    codes = (blocks / scale).astype(np.float32).astype(dtype).astype(np.float64)
    return np.moveaxis((codes * scale).reshape(v.shape), -1, axis)


WIDE = False


def mx_kscale(k):
    if not WIDE:
        return np.ones(k)
    levels = np.array([10, -10, 5, -5, 0])
    if k % 512:
        return np.exp2(np.random.permutation(np.resize(levels, k // 32))).repeat(32)
    a = np.empty((k // 512, 16))
    for p in range(k // 512):
        a[p, :8] = np.random.permutation(np.resize(levels, 8))
        for g in range(8):
            far = levels[np.abs(levels - a[p, g]) >= 10]
            a[p, g + 8] = far[np.random.randint(len(far))]
    return np.exp2(a.ravel()).repeat(32)


def f64(x):
    return np.asarray(x).astype(np.float64)


def striped(idx):
    return np.tile(idx.reshape(-1, 16).T, (8, 1)).astype(np.uint16)


def unstriped(offs):
    return offs[:16].T.reshape(-1).astype(np.int64)


def pack_weight(w):
    k, n = w.shape
    w = f64(np.asarray(w, np.float32).astype(ml_dtypes.bfloat16)).reshape(k // 32, 32, n)
    amax = np.abs(w).max(1)
    byte = np.clip(np.where(amax > 0, np.frexp(amax)[1] - 1 + 127 - 7, 1), 1, 254)
    scaled = (w * np.exp2(127.0 - byte)[:, None, :]).reshape(k, n).astype(np.float32)
    words = np.ascontiguousarray(scaled.reshape(k // 512, 128, 4, n).transpose(0, 1, 3, 2)).astype(ml_dtypes.float8_e4m3fn).view(np.uint8)
    return words, np.ascontiguousarray(byte.astype(np.uint8).reshape(k // 512, 16, n))


def unpack_weight(words, scales):
    g, p, n, _ = words.shape
    vals = np.ascontiguousarray(words).view(ml_dtypes.float8_e4m3fn).astype(np.float64) * np.repeat(np.exp2(scales.astype(np.float64) - 127.0), 8, axis=1)[..., None]
    return vals.transpose(0, 1, 3, 2).reshape(g * 512, n)


E2M1 = np.array([0.0, 0.5, 1.0, 1.5, 2.0, 3.0, 4.0, 6.0, -0.0, -0.5, -1.0, -1.5, -2.0, -3.0, -4.0, -6.0])


def pack_fp4(w):
    k, n = w.shape
    w = f64(np.asarray(w, np.float32).astype(ml_dtypes.bfloat16)).reshape(k // 32, 32, n)
    amax = np.abs(w).max(1)
    mant, ex = np.frexp(amax / 6.0)
    byte = np.clip(np.where(amax > 0, np.where(mant > 0.5, ex, ex - 1) + 127, 1), 1, 254)
    scaled = (w * np.exp2(127.0 - byte)[:, None, :]).reshape(k, n).astype(np.float32)
    c = np.ascontiguousarray(scaled.reshape(k // 512, 128, 4, n).transpose(0, 1, 3, 2)).astype(ml_dtypes.float4_e2m1fn).view(np.uint8) & 0xF
    words = (c[..., 0::2] | (c[..., 1::2] << 4)).reshape(k // 512, 128, 2 * n)
    return np.ascontiguousarray(words), np.ascontiguousarray(byte.astype(np.uint8).reshape(k // 512, 16, n))


def unpack_fp4(words, scales):
    g, _, n = scales.shape
    words = np.ascontiguousarray(words).reshape(g, 128, n, 2)
    nib = np.empty((g, 128, n, 4), np.uint8)
    nib[..., 0::2] = words & 0xF
    nib[..., 1::2] = words >> 4
    vals = E2M1[nib] * np.repeat(np.exp2(scales.astype(np.float64) - 127.0), 8, axis=1)[..., None]
    return vals.transpose(0, 1, 3, 2).reshape(g * 512, n)


def planes(y):
    n, m = y.shape
    v = y.astype(np.float32).astype(ml_dtypes.bfloat16).astype(np.float64).reshape(n // 32, 32, m)
    top = np.abs(v).max(1)
    byte = np.clip(np.where(top > 0, np.frexp(top)[1] - 1 + 127 - 7, 1), 1, 254)
    codes = (v * np.exp2(127.0 - byte)[:, None, :]).reshape(n, m).astype(np.float32).astype(ml_dtypes.float8_e4m3fn).view(np.uint8)
    words = codes.reshape(n // 512, 128, 4, m).transpose(0, 1, 3, 2)
    return np.ascontiguousarray(words), np.ascontiguousarray(byte.astype(np.uint8).reshape(n // 512, 16, m))


def relu(v):
    return np.maximum(v, 0.0)


K, T, S, D, V, H, N, U = 1024, 2048, 1024, 2, 512, 512, 512, 256
P = 2 ** 7


def setup_inputs():
    n = np.random.standard_normal
    s = mx_kscale(K)[:, None]
    u = mx_kscale(H)
    near = np.random.permutation(S)
    next_ = np.random.permutation(V)
    packed_xT = pack_weight(n((K, T)) * s)
    packed_w2 = pack_fp4(n((H, N)) / np.sqrt(H) / u[:, None])
    return {
        "x_words": packed_xT[0],
        "x_scales": packed_xT[1],
        "w1": (n((K, H)) / np.sqrt(K) / s * u).astype(np.float32),
        "w2_words": packed_w2[0],
        "w2_scales": packed_w2[1],
        "gate": (np.tile(np.random.uniform(0.2, 1.0, (D, 1, V)) / np.sqrt(D), (1, P, 1))).astype(np.float32),
        "gate2": (np.tile(np.random.uniform(0.2, 1.0, (D, 1, U)) / np.sqrt(D), (1, P, 1))).astype(np.float32),
        "offs": striped(np.random.permutation(T)[:S]),
        "cen": striped(np.random.permutation(S)[:V]),
        "pos1": striped(near[:V]),
        "pos2": striped(near[V:]),
        "nxt1": striped(next_[:U]),
        "nxt2": striped(next_[U:]),
        "root": striped(np.random.permutation(S)[:U]),
    }


def reference(x_words, x_scales, w1, w2_words, w2_scales, gate, gate2, offs, cen, pos1, pos2, nxt1, nxt2, root):
    xq = unpack_weight(x_words, x_scales)[:, unstriped(offs)]
    h = relu(mxq(f64(w1), 0, "e4m3").T @ xq)
    y = unpack_fp4(w2_words, w2_scales).T @ mxq(h, 0, "e4m3")
    z = 0.8 * (y[:, unstriped(pos1)] * f64(gate)[0, :1] + y[:, unstriped(pos2)] * f64(gate)[1, :1]) + 0.2 * y[:, unstriped(cen)]
    out_0 = 0.8 * (z[:, unstriped(nxt1)] * f64(gate2)[0, :1] + z[:, unstriped(nxt2)] * f64(gate2)[1, :1]) + 0.2 * y[:, unstriped(root)]
    return (out_0,) + planes(out_0)

@@ -1,0 +1,282 @@
+from contextlib import ExitStack
+
+import concourse.mybir as mybir
+from concourse.masks import make_identity
+
+K, T, S, V, H, N, U = 1024, 2048, 1024, 512, 512, 512, 256
+FLOPS = 2 * K * H * S + 2 * H * N * S
+
+F32 = mybir.dt.float32
+BF16 = mybir.dt.bfloat16
+I32 = mybir.dt.int32
+U32 = mybir.dt.uint32
+U16 = mybir.dt.uint16
+U8 = mybir.dt.uint8
+FP8X4 = mybir.dt.float8_e4m3fn_x4
+FP4X4 = mybir.dt.float4_e2m1fn_x4
+ACT = mybir.ActivationFunctionType
+ALU = mybir.AluOpType
+
+P = 128
+PACK = 4
+PASSES = K // (P * PACK)
+CHUNK = 128
+CHUNKS = S // CHUNK
+MIX = 0.8
+KEEP = 0.2
+
+
+def tile_picked_zappnp_relu_po_kernel(
+    tc, x_words, x_scales, w1, w2_words, w2_scales, gate, gate2,
+    offs, cen, pos1, pos2, nxt1, nxt2, root, out_0, out_1, out_2,
+):
+    nc = tc.nc
+    with ExitStack() as ctx:
+        held = ctx.enter_context(tc.tile_pool(name="held", bufs=1))
+        psum = ctx.enter_context(tc.psum_pool(name="psum", bufs=1))
+
+        def load_list(name, ap):
+            lst = held.tile(list(ap.shape), U16, name=name)
+            nc.sync.dma_start(lst[:], ap)
+            return lst
+
+        def load_w1(o):
+            raw = held.tile([P, PACK, H], F32, name=f"w1_raw{o}")
+            nc.sync.dma_start(out=raw[:], in_=w1[o * 512:(o + 1) * 512, :].rearrange("(p j) c -> p j c", j=PACK))
+            return raw
+
+        def load_x(o):
+            xw = held.tile([P, T], I32, name=f"x_table{o}")
+            nc.sync.dma_start(out=xw[:], in_=x_words[o].rearrange("p n t -> p (n t)").bitcast(I32))
+            return xw
+
+        xs_table = held.tile([P, T], U8, name="xs_table", align_bytes=64)
+        nc.vector.memset(xs_table[:].bitcast(I32), 0)
+        w2s_raw = held.tile([P, N], U8, name="w2s_raw", align_bytes=64)
+        nc.gpsimd.memset(w2s_raw[:].bitcast(I32), 0)
+
+        offs_t = load_list("offs_t", offs)
+        w1_raw = [load_w1(0)]
+        for q in range(4):
+            nc.sync.dma_start(out=xs_table[32 * q:32 * q + 4 * PASSES, :].bitcast(I32),
+                              in_=x_scales[:, 4 * q:4 * q + 4, :].bitcast(I32))
+        x_table = [load_x(0)]
+        w2w_raw = held.tile([P, 2 * N], U8, name="w2w_raw", align_bytes=64)
+        nc.sync.dma_start(out=w2w_raw[:].bitcast(I32), in_=w2_words[0].bitcast(I32))
+        w1_raw.append(load_w1(1))
+        x_table.append(load_x(1))
+        pos1_t = load_list("pos1_t", pos1)
+        pos2_t = load_list("pos2_t", pos2)
+        cen_t = load_list("cen_t", cen)
+        gate_t = held.tile([P, 2, V], F32, name="gate_t")
+        nc.sync.dma_start(out=gate_t[:], in_=gate.rearrange("d p v -> p d v"))
+        nxt1_t = load_list("nxt1_t", nxt1)
+        nxt2_t = load_list("nxt2_t", nxt2)
+        root_t = load_list("root_t", root)
+        gate2_t = held.tile([P, 2, U], F32, name="gate2_t")
+        nc.sync.dma_start(out=gate2_t[:], in_=gate2.rearrange("d p v -> p d v"))
+
+        for q in range(4):
+            nc.gpsimd.dma_start(out=w2s_raw[32 * q:32 * q + 4, :].bitcast(I32),
+                                in_=w2_scales[0, 4 * q:4 * q + 4, :].bitcast(I32))
+        w2s = held.tile([P, N], U8, name="w2s", align_bytes=64)
+        nc.gpsimd.tensor_copy(out=w2s[:].rearrange("p (t m) -> p t m", t=PACK),
+                              in_=w2s_raw[:].rearrange("p (m t) -> p t m", t=PACK))
+
+        ident = held.tile([P, P], F32, name="ident")
+        make_identity(nc, ident[:])
+
+        w1_bf = [held.tile([P, PACK * H], BF16, name=f"w1_bf{o}", align_bytes=64) for o in range(PASSES)]
+        w1_codes = [held.tile([P, H], U32, name=f"w1_codes{o}", align_bytes=64) for o in range(PASSES)]
+        w1_scales = [held.tile([P, H], U8, name=f"w1_scales{o}", align_bytes=64) for o in range(PASSES)]
+        x_codes = [held.tile([P, S], U32, name=f"x_codes{o}", align_bytes=64) for o in range(PASSES)]
+        x_sc = held.tile([P, S], U8, name="x_sc", align_bytes=64)
+
+        def cast_w1(o, copy, lo, hi):
+            copy(out=w1_bf[o][:].rearrange("p (t m j) -> p m t j", t=PACK, j=PACK)[:, lo:hi],
+                 in_=w1_raw[o][:].rearrange("p j (m t) -> p m t j", t=PACK)[:, lo:hi])
+
+        def quantize_w1(o):
+            nc.vector.quantize_mx(out=w1_codes[o][:].bitcast(FP8X4), scales=w1_scales[o][:], in_=w1_bf[o][:])
+
+        def gather_x(o, lo, hi):
+            nc.vector.tensor_copy(x_codes[o][:, lo:hi],
+                                  x_table[o][:].bitcast(U32).indirect(offs_t[:, lo // 16:hi // 16]))
+
+        banks = [psum.tile([P, PACK, CHUNK], F32, name=f"h_bank{c}", tag=f"bank{c}") for c in range(CHUNKS)]
+
+        def layer1(o, c):
+            cols = slice(c * CHUNK, (c + 1) * CHUNK)
+            for t in range(PACK):
+                nc.tensor.matmul_mx(
+                    out=banks[c][:, t, :],
+                    lhsT=w1_codes[o][:, t * P:(t + 1) * P].bitcast(FP8X4),
+                    lhsT_scale=w1_scales[o][:, t * P:(t + 1) * P],
+                    rhs=x_codes[o][:, cols].bitcast(FP8X4),
+                    rhs_scale=x_sc[4 * o:P, cols],
+                    start=(o == 0 and t == 0),
+                    stop=(o == PASSES - 1 and t == PACK - 1),
+                )
+
+        nc.vector.tensor_copy(x_sc[:], xs_table[:].indirect(offs_t[:]))
+        cast_w1(0, nc.scalar.copy, 0, P)
+        gather_x(0, 0, 512)
+        quantize_w1(0)
+        gather_x(0, 512, 1024)
+        w2w = held.tile([P, 2 * N], U8, name="w2w", align_bytes=64)
+        nc.scalar.copy(out=w2w[:].bitcast(U16).rearrange("p (t m) -> p t m", t=PACK),
+                       in_=w2w_raw[:].bitcast(U16).rearrange("p (m t) -> p t m", t=PACK))
+        for c in range(CHUNKS):
+            layer1(0, c)
+        cast_w1(1, nc.scalar.copy, 0, P // 2)
+        cast_w1(1, nc.vector.tensor_copy, P // 2, P)
+        quantize_w1(1)
+
+        h_bf = held.tile([P, PACK * S], BF16, name="h_bf", align_bytes=64)
+        h_codes = held.tile([P, S], U32, name="h_codes", align_bytes=64)
+        h_scales = held.tile([P, S], U8, name="h_scales", align_bytes=64)
+
+        def relu(c, on_vector):
+            dst = h_bf[:, c * 512:(c + 1) * 512].rearrange("p (n t) -> p n t", t=PACK)
+            src = banks[c][:].rearrange("p t n -> p n t")
+            if on_vector:
+                nc.vector.tensor_scalar_max(dst, src, 0.0)
+            else:
+                nc.scalar.activation(dst, src, ACT.Relu)
+
+        def quantize_h(k):
+            cols = slice(256 * k, 256 * (k + 1))
+            nc.vector.quantize_mx(out=h_codes[:, cols].bitcast(FP8X4), scales=h_scales[:, cols],
+                                  in_=h_bf[:, 1024 * k:1024 * (k + 1)])
+
+        for k in range(4):
+            gather_x(1, 256 * k, 256 * (k + 1))
+            layer1(1, 2 * k)
+            layer1(1, 2 * k + 1)
+        for c in (0, 1, 2, 3, 4):
+            relu(c, False)
+        quantize_h(0)
+        relu(5, True)
+        quantize_h(1)
+        relu(6, True)
+        relu(7, False)
+        quantize_h(2)
+        quantize_h(3)
+
+        y_bank = {}
+        for half in range(2):
+            for t in range(PACK):
+                y_bank[t, half] = psum.tile([P, 512], F32, name=f"y_bank{t}_{half}", tag=f"bank{4 * half + t}")
+
+        def layer2(t, k):
+            cols = slice(256 * k, 256 * (k + 1))
+            nc.tensor.matmul_mx(
+                out=y_bank[t, k // 2][:, 256 * (k % 2):256 * (k % 2 + 1)],
+                lhsT=w2w[:, 2 * P * t:2 * P * (t + 1)].bitcast(FP4X4),
+                lhsT_scale=w2s[:, P * t:P * (t + 1)],
+                rhs=h_codes[:, cols].bitcast(FP8X4),
+                rhs_scale=h_scales[:, cols],
+                start=True, stop=True,
+            )
+
+        for k in range(4):
+            for t in range(PACK):
+                layer2(t, k)
+
+        y = [held.tile([P, S], F32, name=f"y{t}") for t in range(PACK)]
+        z = [held.tile([P, V], F32, name=f"z{t}") for t in range(PACK)]
+        res = held.tile([P, PACK, U], F32, name="res")
+        out_rows = out_0.rearrange("(p t) x -> p t x", t=PACK)
+
+        def empty_y(t, half, copy):
+            copy(out=y[t][:, 512 * half:512 * (half + 1)], in_=y_bank[t, half][:])
+
+        def own(window, lst, n, scale, name):
+            c = held.tile([P, n], F32, name=name)
+            nc.scalar.activation(c[:], window[:].indirect(lst[:]), ACT.Copy, scale=scale)
+            return c
+
+        def near(window, lst, weights, n, name):
+            a = held.tile([P, n], F32, name=name)
+            nc.vector.tensor_tensor(a[:], window[:].indirect(lst[:]), weights, ALU.mult)
+            return a
+
+        def turn(bank, term, first, last):
+            for blk in range(PACK):
+                cols = slice(blk * P, (blk + 1) * P)
+                nc.tensor.matmul(bank[:, cols], lhsT=term[:, cols], rhs=ident[:], is_transpose=True,
+                                 start=(first and blk == 0), stop=(last and blk == PACK - 1))
+
+        sum_bank, back_bank, z_turned, own2 = {}, {}, {}, {}
+
+        def mix1_gathers(t):
+            c1 = own(y[t], cen_t, V, KEEP / MIX, f"own1_{t}")
+            a1 = near(y[t], pos1_t, gate_t[:, 0, :], V, f"a1_{t}")
+            b1 = near(y[t], pos2_t, gate_t[:, 1, :], V, f"b1_{t}")
+            sum_bank[t] = psum.tile([P, V], F32, name=f"sum_bank{t}", tag=f"bank{t}")
+            turn(sum_bank[t], a1, True, False)
+            turn(sum_bank[t], c1, False, False)
+            turn(sum_bank[t], b1, False, True)
+
+        def mix1_scale(t):
+            z_turned[t] = held.tile([P, V], F32, name=f"z_turned{t}")
+            nc.scalar.activation(z_turned[t][:], sum_bank[t][:], ACT.Copy, scale=MIX)
+            back_bank[t] = psum.tile([P, V], F32, name=f"back_bank{t}", tag=f"bank{4 + t}")
+            turn(back_bank[t], z_turned[t], True, True)
+
+        def mix1_out(t):
+            nc.scalar.copy(out=z[t][:], in_=back_bank[t][:])
+
+        def mix2_own(t):
+            own2[t] = own(y[t], root_t, U, KEEP, f"own2_{t}")
+
+        def mix2_near(t):
+            return (near(z[t], nxt1_t, gate2_t[:, 0, :], U, f"a2_{t}"),
+                    near(z[t], nxt2_t, gate2_t[:, 1, :], U, f"b2_{t}"))
+
+        def mix2_sum(t, terms):
+            s = held.tile([P, U], F32, name=f"s2_{t}")
+            nc.vector.tensor_tensor(s[:], terms[0][:], terms[1][:], ALU.add)
+            return s
+
+        def mix2_out(t, s):
+            nc.vector.scalar_tensor_tensor(res[:, t, :], s[:], MIX, own2[t][:], ALU.mult, ALU.add)
+            nc.sync.dma_start(out=out_rows[:, t, :], in_=res[:, t, :])
+
+        empty_y(0, 0, nc.scalar.copy)
+        empty_y(0, 1, nc.vector.tensor_copy)
+        for t in range(PACK):
+            if t + 1 < PACK:
+                empty_y(t + 1, 0, nc.scalar.copy)
+                empty_y(t + 1, 1, nc.scalar.copy)
+            if t >= 2:
+                mix1_scale(t - 2)
+            mix1_gathers(t)
+            if t >= 2:
+                mix1_out(t - 2)
+        mix2_own(0)
+        mix1_scale(2)
+        mix2_own(1)
+        mix1_out(2)
+        mix1_scale(3)
+        mix2_own(2)
+        mix1_out(3)
+        mix2_own(3)
+        terms = mix2_near(0)
+        for t in range(PACK):
+            s = mix2_sum(t, terms)
+            if t + 1 < PACK:
+                terms = mix2_near(t + 1)
+            mix2_out(t, s)
+
+        res_bf = held.tile([P, PACK * U], BF16, name="res_bf", align_bytes=64)
+        res_codes = held.tile([P, U], U32, name="res_codes", align_bytes=64)
+        res_scales = held.tile([P, U], U8, name="res_scales", align_bytes=64)
+        nc.vector.tensor_copy(out=res_bf[:].rearrange("p (x t) -> p x t", t=PACK),
+                              in_=res[:].rearrange("p t x -> p x t"))
+        nc.vector.quantize_mx(out=res_codes[:].bitcast(FP8X4), scales=res_scales[:], in_=res_bf[:])
+        nc.sync.dma_start(out=out_1[0].rearrange("p n t -> p (n t)").bitcast(I32), in_=res_codes[:].bitcast(I32))
+        for q in range(4):
+            queue = nc.scalar if q % 2 == 0 else nc.sync
+            queue.dma_start(out=out_2[0, 4 * q:4 * q + 4, :].bitcast(I32),
+                            in_=res_scales[32 * q:32 * q + 4, :].bitcast(I32))

@@ -63,6 +63,9 @@ def tile_picked_zappnp_relu_po_kernel(
         x_table = [load_x(0)]
         w2w_raw = held.tile([P, 2 * N], U8, name="w2w_raw", align_bytes=64)
         nc.sync.dma_start(out=w2w_raw[:].bitcast(I32), in_=w2_words[0].bitcast(I32))
+        for q in range(4):
+            nc.sync.dma_start(out=w2s_raw[32 * q:32 * q + 4, :].bitcast(I32),
+                              in_=w2_scales[0, 4 * q:4 * q + 4, :].bitcast(I32))
         w1_raw.append(load_w1(1))
         x_table.append(load_x(1))
         pos1_t = load_list("pos1_t", pos1)
@@ -76,12 +79,7 @@ def tile_picked_zappnp_relu_po_kernel(
         gate2_t = held.tile([P, 2, U], F32, name="gate2_t")
         nc.sync.dma_start(out=gate2_t[:], in_=gate2.rearrange("d p v -> p d v"))
 
-        for q in range(4):
-            nc.gpsimd.dma_start(out=w2s_raw[32 * q:32 * q + 4, :].bitcast(I32),
-                                in_=w2_scales[0, 4 * q:4 * q + 4, :].bitcast(I32))
         w2s = held.tile([P, N], U8, name="w2s", align_bytes=64)
-        nc.gpsimd.tensor_copy(out=w2s[:].rearrange("p (t m) -> p t m", t=PACK),
-                              in_=w2s_raw[:].rearrange("p (m t) -> p t m", t=PACK))
 
         ident = held.tile([P, P], F32, name="ident")
         make_identity(nc, ident[:])
@@ -118,18 +116,21 @@ def tile_picked_zappnp_relu_po_kernel(
                     stop=(o == PASSES - 1 and t == PACK - 1),
                 )
 
+        cast_w1(0, nc.scalar.copy, 0, 96)
+        cast_w1(0, nc.vector.tensor_copy, 96, P)
         nc.vector.tensor_copy(x_sc[:], xs_table[:].indirect(offs_t[:]))
-        cast_w1(0, nc.scalar.copy, 0, P)
-        gather_x(0, 0, 512)
         quantize_w1(0)
-        gather_x(0, 512, 1024)
+        for lo, hi in ((0, 256), (256, 512), (512, 1024)):
+            gather_x(0, lo, hi)
         w2w = held.tile([P, 2 * N], U8, name="w2w", align_bytes=64)
         nc.scalar.copy(out=w2w[:].bitcast(U16).rearrange("p (t m) -> p t m", t=PACK),
                        in_=w2w_raw[:].bitcast(U16).rearrange("p (m t) -> p t m", t=PACK))
         for c in range(CHUNKS):
             layer1(0, c)
-        cast_w1(1, nc.scalar.copy, 0, P // 2)
-        cast_w1(1, nc.vector.tensor_copy, P // 2, P)
+        nc.vector.tensor_copy(out=w2s[:].rearrange("p (t m) -> p t m", t=PACK),
+                              in_=w2s_raw[:].rearrange("p (m t) -> p t m", t=PACK))
+        cast_w1(1, nc.scalar.copy, 0, 96)
+        cast_w1(1, nc.vector.tensor_copy, 96, P)
         quantize_w1(1)
 
         h_bf = held.tile([P, PACK * S], BF16, name="h_bf", align_bytes=64)
@@ -153,25 +154,22 @@ def tile_picked_zappnp_relu_po_kernel(
             gather_x(1, 256 * k, 256 * (k + 1))
             layer1(1, 2 * k)
             layer1(1, 2 * k + 1)
-        for c in (0, 1, 2, 3, 4):
-            relu(c, False)
-        quantize_h(0)
-        relu(5, True)
-        quantize_h(1)
-        relu(6, True)
-        relu(7, False)
-        quantize_h(2)
-        quantize_h(3)
+        for k in range(4):
+            relu(2 * k, k >= 2)
+            relu(2 * k + 1, False)
+            quantize_h(k)
 
-        y_bank = {}
-        for half in range(2):
-            for t in range(PACK):
-                y_bank[t, half] = psum.tile([P, 512], F32, name=f"y_bank{t}_{half}", tag=f"bank{4 * half + t}")
+        y_bank = [psum.tile([P, 512], F32, name=f"y_bank{c}", tag=f"bank{c}") for c in range(CHUNKS)]
+
+        def y_place(t, k):
+            if k >= 2 and t in (0, PACK - 1):
+                return y_bank[4 if k == 2 else 7][:, 256 * (t > 0):256 * (t > 0) + 256]
+            return y_bank[4 * (k // 2) + t][:, 256 * (k % 2):256 * (k % 2 + 1)]
 
         def layer2(t, k):
             cols = slice(256 * k, 256 * (k + 1))
             nc.tensor.matmul_mx(
-                out=y_bank[t, k // 2][:, 256 * (k % 2):256 * (k % 2 + 1)],
+                out=y_place(t, k),
                 lhsT=w2w[:, 2 * P * t:2 * P * (t + 1)].bitcast(FP4X4),
                 lhsT_scale=w2s[:, P * t:P * (t + 1)],
                 rhs=h_codes[:, cols].bitcast(FP8X4),
@@ -179,17 +177,34 @@ def tile_picked_zappnp_relu_po_kernel(
                 start=True, stop=True,
             )
 
-        for k in range(4):
-            for t in range(PACK):
-                layer2(t, k)
-
         y = [held.tile([P, S], F32, name=f"y{t}") for t in range(PACK)]
         z = [held.tile([P, V], F32, name=f"z{t}") for t in range(PACK)]
         res = held.tile([P, PACK, U], F32, name="res")
         out_rows = out_0.rearrange("(p t) x -> p t x", t=PACK)
 
-        def empty_y(t, half, copy):
-            copy(out=y[t][:, 512 * half:512 * (half + 1)], in_=y_bank[t, half][:])
+        def scaled(dst, src, scale):
+            nc.scalar.activation(dst, src, ACT.Copy, scale=scale)
+
+        def empty_quarter(t, k):
+            scaled(y[t][:, 256 * k:256 * (k + 1)], y_place(t, k), KEEP)
+
+        def empty_y(t):
+            scaled(y[t][:, 0:512], y_bank[t][:], KEEP)
+            if t == PACK - 1:
+                empty_quarter(t, 2)
+                empty_quarter(t, 3)
+            elif t > 0:
+                scaled(y[t][:, 512:1024], y_bank[4 + t][:], KEEP)
+
+        for k in range(3):
+            for t in range(PACK):
+                layer2(t, k)
+        empty_y(0)
+        empty_quarter(0, 2)
+        for t in range(PACK - 1):
+            layer2(t, 3)
+        nc.vector.tensor_scalar_mul(y[0][:, 768:1024], y_place(0, 3), KEEP)
+        layer2(PACK - 1, 3)
 
         def own(window, lst, n, scale, name):
             c = held.tile([P, n], F32, name=name)
@@ -202,10 +217,11 @@ def tile_picked_zappnp_relu_po_kernel(
             return a
 
         def turn(bank, term, first, last):
-            for blk in range(PACK):
+            blocks = term.shape[1] // P
+            for blk in range(blocks):
                 cols = slice(blk * P, (blk + 1) * P)
                 nc.tensor.matmul(bank[:, cols], lhsT=term[:, cols], rhs=ident[:], is_transpose=True,
-                                 start=(first and blk == 0), stop=(last and blk == PACK - 1))
+                                 start=(first and blk == 0), stop=(last and blk == blocks - 1))
 
         sum_bank, back_bank, z_turned, own2 = {}, {}, {}, {}
 
@@ -220,7 +236,7 @@ def tile_picked_zappnp_relu_po_kernel(
 
         def mix1_scale(t):
             z_turned[t] = held.tile([P, V], F32, name=f"z_turned{t}")
-            nc.scalar.activation(z_turned[t][:], sum_bank[t][:], ACT.Copy, scale=MIX)
+            scaled(z_turned[t][:], sum_bank[t][:], MIX * MIX / KEEP)
             back_bank[t] = psum.tile([P, V], F32, name=f"back_bank{t}", tag=f"bank{4 + t}")
             turn(back_bank[t], z_turned[t], True, True)
 
@@ -228,52 +244,68 @@ def tile_picked_zappnp_relu_po_kernel(
             nc.scalar.copy(out=z[t][:], in_=back_bank[t][:])
 
         def mix2_own(t):
-            own2[t] = own(y[t], root_t, U, KEEP, f"own2_{t}")
+            own2[t] = own(y[t], root_t, U, 1.0, f"own2_{t}")
 
         def mix2_near(t):
             return (near(z[t], nxt1_t, gate2_t[:, 0, :], U, f"a2_{t}"),
                     near(z[t], nxt2_t, gate2_t[:, 1, :], U, f"b2_{t}"))
 
-        def mix2_sum(t, terms):
-            s = held.tile([P, U], F32, name=f"s2_{t}")
-            nc.vector.tensor_tensor(s[:], terms[0][:], terms[1][:], ALU.add)
-            return s
-
-        def mix2_out(t, s):
-            nc.vector.scalar_tensor_tensor(res[:, t, :], s[:], MIX, own2[t][:], ALU.mult, ALU.add)
+        def store(t):
             nc.sync.dma_start(out=out_rows[:, t, :], in_=res[:, t, :])
 
-        empty_y(0, 0, nc.scalar.copy)
-        empty_y(0, 1, nc.vector.tensor_copy)
+        def mix2_turned(t, terms):
+            bank = psum.tile([P, U], F32, name=f"sum2_bank{t}", tag=f"bank{t}")
+            turn(bank, own2[t], True, False)
+            turn(bank, terms[0], False, False)
+            turn(bank, terms[1], False, True)
+            turned = held.tile([P, U], F32, name=f"res_turned{t}")
+            nc.scalar.copy(out=turned[:], in_=bank[:])
+            back = psum.tile([P, U], F32, name=f"back2_bank{t}", tag=f"bank{4 + t}")
+            turn(back, turned, True, True)
+            nc.scalar.copy(out=res[:, t, :], in_=back[:])
+            store(t)
+
+        def mix2_part(t, a):
+            s = held.tile([P, U], F32, name=f"s2_{t}")
+            nc.vector.tensor_tensor(s[:], y[t][:].indirect(root_t[:]), a[:], ALU.add)
+            return s
+
+        def mix2_out(t, b, s):
+            nc.vector.tensor_tensor(res[:, t, :], b[:], s[:], ALU.add)
+            store(t)
+
         for t in range(PACK):
             if t + 1 < PACK:
-                empty_y(t + 1, 0, nc.scalar.copy)
-                empty_y(t + 1, 1, nc.scalar.copy)
+                empty_y(t + 1)
             if t >= 2:
                 mix1_scale(t - 2)
             mix1_gathers(t)
             if t >= 2:
                 mix1_out(t - 2)
-        mix2_own(0)
         mix1_scale(2)
-        mix2_own(1)
+        mix2_own(0)
+        terms0 = mix2_near(0)
         mix1_out(2)
         mix1_scale(3)
-        mix2_own(2)
+        mix2_own(1)
+        terms1 = mix2_near(1)
         mix1_out(3)
-        mix2_own(3)
-        terms = mix2_near(0)
-        for t in range(PACK):
-            s = mix2_sum(t, terms)
-            if t + 1 < PACK:
-                terms = mix2_near(t + 1)
-            mix2_out(t, s)
+        mix2_turned(0, terms0)
+        mix2_turned(1, terms1)
+        terms2 = mix2_near(2)
+        part2 = mix2_part(2, terms2[0])
+        a3 = near(z[3], nxt1_t, gate2_t[:, 0, :], U, "a2_3")
+        mix2_out(2, terms2[1], part2)
+        b3 = near(z[3], nxt2_t, gate2_t[:, 1, :], U, "b2_3")
+        part3 = mix2_part(3, a3)
+        mix2_out(3, b3, part3)
 
         res_bf = held.tile([P, PACK * U], BF16, name="res_bf", align_bytes=64)
         res_codes = held.tile([P, U], U32, name="res_codes", align_bytes=64)
         res_scales = held.tile([P, U], U8, name="res_scales", align_bytes=64)
-        nc.vector.tensor_copy(out=res_bf[:].rearrange("p (x t) -> p x t", t=PACK),
-                              in_=res[:].rearrange("p t x -> p x t"))
+        for copy, lo, hi in ((nc.scalar.copy, 0, 96), (nc.vector.tensor_copy, 96, U)):
+            copy(out=res_bf[:].rearrange("p (x t) -> p x t", t=PACK)[:, lo:hi],
+                 in_=res[:].rearrange("p t x -> p x t")[:, lo:hi])
         nc.vector.quantize_mx(out=res_codes[:].bitcast(FP8X4), scales=res_scales[:], in_=res_bf[:])
         nc.sync.dma_start(out=out_1[0].rearrange("p n t -> p (n t)").bitcast(I32), in_=res_codes[:].bitcast(I32))
         for q in range(4):

@@ -19,11 +19,19 @@ ALU = mybir.AluOpType
 
 P = 128
 PACK = 4
-PASSES = K // (P * PACK)
-CHUNK = 128
+K_PASS = P * PACK
+PASSES = K // K_PASS
+QUADRANTS = 4
+BANK = 512
+CHUNK = BANK // PACK
 CHUNKS = S // CHUNK
+QUARTER = S // 4
+LIST_ROWS = 16
 MIX = 0.8
 KEEP = 0.2
+
+W1_SHARE = (96, 64)
+OUT_SHARE = 96
 
 
 def tile_picked_zappnp_relu_po_kernel(
@@ -35,20 +43,22 @@ def tile_picked_zappnp_relu_po_kernel(
         held = ctx.enter_context(tc.tile_pool(name="held", bufs=1))
         psum = ctx.enter_context(tc.psum_pool(name="psum", bufs=1))
 
-        def load_list(name, ap):
-            lst = held.tile(list(ap.shape), U16, name=name)
-            nc.sync.dma_start(lst[:], ap)
+
+        def load_list(name, entries):
+            lst = held.tile(list(entries.shape), U16, name=name)
+            nc.sync.dma_start(lst[:], entries)
             return lst
 
         def load_w1(o):
             raw = held.tile([P, PACK, H], F32, name=f"w1_raw{o}")
-            nc.sync.dma_start(out=raw[:], in_=w1[o * 512:(o + 1) * 512, :].rearrange("(p j) c -> p j c", j=PACK))
+            rows = w1[o * K_PASS:(o + 1) * K_PASS, :]
+            nc.sync.dma_start(out=raw[:], in_=rows.rearrange("(p j) c -> p j c", j=PACK))
             return raw
 
         def load_x(o):
-            xw = held.tile([P, T], I32, name=f"x_table{o}")
-            nc.sync.dma_start(out=xw[:], in_=x_words[o].rearrange("p n t -> p (n t)").bitcast(I32))
-            return xw
+            table = held.tile([P, T], I32, name=f"x_table{o}")
+            nc.sync.dma_start(out=table[:], in_=x_words[o].rearrange("p n t -> p (n t)").bitcast(I32))
+            return table
 
         xs_table = held.tile([P, T], U8, name="xs_table", align_bytes=64)
         nc.vector.memset(xs_table[:].bitcast(I32), 0)
@@ -57,17 +67,17 @@ def tile_picked_zappnp_relu_po_kernel(
 
         offs_t = load_list("offs_t", offs)
         w1_raw = [load_w1(0)]
-        for q in range(4):
+        for q in range(QUADRANTS):
             nc.sync.dma_start(out=xs_table[32 * q:32 * q + 4 * PASSES, :].bitcast(I32),
                               in_=x_scales[:, 4 * q:4 * q + 4, :].bitcast(I32))
         x_table = [load_x(0)]
-        w2w_raw = held.tile([P, 2 * N], U8, name="w2w_raw", align_bytes=64)
-        nc.sync.dma_start(out=w2w_raw[:].bitcast(I32), in_=w2_words[0].bitcast(I32))
-        for q in range(4):
-            nc.sync.dma_start(out=w2s_raw[32 * q:32 * q + 4, :].bitcast(I32),
-                              in_=w2_scales[0, 4 * q:4 * q + 4, :].bitcast(I32))
+        for q in range(QUADRANTS):
+            nc.gpsimd.dma_start(out=w2s_raw[32 * q:32 * q + 4, :].bitcast(I32),
+                                in_=w2_scales[0, 4 * q:4 * q + 4, :].bitcast(I32))
         w1_raw.append(load_w1(1))
         x_table.append(load_x(1))
+        w2w_raw = held.tile([P, 2 * N], U8, name="w2w_raw", align_bytes=64)
+        nc.sync.dma_start(out=w2w_raw[:].bitcast(I32), in_=w2_words[0].bitcast(I32))
         pos1_t = load_list("pos1_t", pos1)
         pos2_t = load_list("pos2_t", pos2)
         cen_t = load_list("cen_t", cen)
@@ -80,9 +90,12 @@ def tile_picked_zappnp_relu_po_kernel(
         nc.sync.dma_start(out=gate2_t[:], in_=gate2.rearrange("d p v -> p d v"))
 
         w2s = held.tile([P, N], U8, name="w2s", align_bytes=64)
+        nc.gpsimd.tensor_copy(out=w2s[:].rearrange("p (t m) -> p t m", t=PACK),
+                              in_=w2s_raw[:].rearrange("p (m t) -> p t m", t=PACK))
 
         ident = held.tile([P, P], F32, name="ident")
         make_identity(nc, ident[:])
+
 
         w1_bf = [held.tile([P, PACK * H], BF16, name=f"w1_bf{o}", align_bytes=64) for o in range(PASSES)]
         w1_codes = [held.tile([P, H], U32, name=f"w1_codes{o}", align_bytes=64) for o in range(PASSES)]
@@ -90,24 +103,27 @@ def tile_picked_zappnp_relu_po_kernel(
         x_codes = [held.tile([P, S], U32, name=f"x_codes{o}", align_bytes=64) for o in range(PASSES)]
         x_sc = held.tile([P, S], U8, name="x_sc", align_bytes=64)
 
-        def cast_w1(o, copy, lo, hi):
-            copy(out=w1_bf[o][:].rearrange("p (t m j) -> p m t j", t=PACK, j=PACK)[:, lo:hi],
-                 in_=w1_raw[o][:].rearrange("p j (m t) -> p m t j", t=PACK)[:, lo:hi])
+        def round_w1(o):
+            dst = w1_bf[o][:].rearrange("p (t m j) -> p m t j", t=PACK, j=PACK)
+            src = w1_raw[o][:].rearrange("p j (m t) -> p m t j", t=PACK)
+            share = W1_SHARE[o]
+            nc.scalar.copy(out=dst[:, 0:share], in_=src[:, 0:share])
+            nc.vector.tensor_copy(out=dst[:, share:P], in_=src[:, share:P])
 
         def quantize_w1(o):
             nc.vector.quantize_mx(out=w1_codes[o][:].bitcast(FP8X4), scales=w1_scales[o][:], in_=w1_bf[o][:])
 
         def gather_x(o, lo, hi):
-            nc.vector.tensor_copy(x_codes[o][:, lo:hi],
-                                  x_table[o][:].bitcast(U32).indirect(offs_t[:, lo // 16:hi // 16]))
+            entries = offs_t[:, lo // LIST_ROWS:hi // LIST_ROWS]
+            nc.vector.tensor_copy(x_codes[o][:, lo:hi], x_table[o][:].bitcast(U32).indirect(entries))
 
-        banks = [psum.tile([P, PACK, CHUNK], F32, name=f"h_bank{c}", tag=f"bank{c}") for c in range(CHUNKS)]
+        h_bank = [psum.tile([P, PACK, CHUNK], F32, name=f"h_bank{c}", tag=f"bank{c}") for c in range(CHUNKS)]
 
         def layer1(o, c):
             cols = slice(c * CHUNK, (c + 1) * CHUNK)
             for t in range(PACK):
                 nc.tensor.matmul_mx(
-                    out=banks[c][:, t, :],
+                    out=h_bank[c][:, t, :],
                     lhsT=w1_codes[o][:, t * P:(t + 1) * P].bitcast(FP8X4),
                     lhsT_scale=w1_scales[o][:, t * P:(t + 1) * P],
                     rhs=x_codes[o][:, cols].bitcast(FP8X4),
@@ -116,58 +132,58 @@ def tile_picked_zappnp_relu_po_kernel(
                     stop=(o == PASSES - 1 and t == PACK - 1),
                 )
 
-        cast_w1(0, nc.scalar.copy, 0, 96)
-        cast_w1(0, nc.vector.tensor_copy, 96, P)
+        round_w1(0)
         nc.vector.tensor_copy(x_sc[:], xs_table[:].indirect(offs_t[:]))
         quantize_w1(0)
-        for lo, hi in ((0, 256), (256, 512), (512, 1024)):
+        for lo, hi in ((0, QUARTER), (QUARTER, 2 * QUARTER), (2 * QUARTER, S)):
             gather_x(0, lo, hi)
+        for c in range(CHUNKS):
+            layer1(0, c)
+        round_w1(1)
+        quantize_w1(1)
+
         w2w = held.tile([P, 2 * N], U8, name="w2w", align_bytes=64)
         nc.scalar.copy(out=w2w[:].bitcast(U16).rearrange("p (t m) -> p t m", t=PACK),
                        in_=w2w_raw[:].bitcast(U16).rearrange("p (m t) -> p t m", t=PACK))
-        for c in range(CHUNKS):
-            layer1(0, c)
-        nc.vector.tensor_copy(out=w2s[:].rearrange("p (t m) -> p t m", t=PACK),
-                              in_=w2s_raw[:].rearrange("p (m t) -> p t m", t=PACK))
-        cast_w1(1, nc.scalar.copy, 0, 96)
-        cast_w1(1, nc.vector.tensor_copy, 96, P)
-        quantize_w1(1)
 
         h_bf = held.tile([P, PACK * S], BF16, name="h_bf", align_bytes=64)
         h_codes = held.tile([P, S], U32, name="h_codes", align_bytes=64)
         h_scales = held.tile([P, S], U8, name="h_scales", align_bytes=64)
 
         def relu(c, on_vector):
-            dst = h_bf[:, c * 512:(c + 1) * 512].rearrange("p (n t) -> p n t", t=PACK)
-            src = banks[c][:].rearrange("p t n -> p n t")
+            dst = h_bf[:, c * BANK:(c + 1) * BANK].rearrange("p (n t) -> p n t", t=PACK)
+            src = h_bank[c][:].rearrange("p t n -> p n t")
             if on_vector:
                 nc.vector.tensor_scalar_max(dst, src, 0.0)
             else:
                 nc.scalar.activation(dst, src, ACT.Relu)
 
         def quantize_h(k):
-            cols = slice(256 * k, 256 * (k + 1))
+            cols = slice(QUARTER * k, QUARTER * (k + 1))
             nc.vector.quantize_mx(out=h_codes[:, cols].bitcast(FP8X4), scales=h_scales[:, cols],
-                                  in_=h_bf[:, 1024 * k:1024 * (k + 1)])
+                                  in_=h_bf[:, PACK * QUARTER * k:PACK * QUARTER * (k + 1)])
 
         for k in range(4):
-            gather_x(1, 256 * k, 256 * (k + 1))
+            gather_x(1, QUARTER * k, QUARTER * (k + 1))
             layer1(1, 2 * k)
             layer1(1, 2 * k + 1)
         for k in range(4):
-            relu(2 * k, k >= 2)
-            relu(2 * k + 1, False)
+            relu(2 * k, on_vector=k >= 2)
+            relu(2 * k + 1, on_vector=False)
             quantize_h(k)
 
-        y_bank = [psum.tile([P, 512], F32, name=f"y_bank{c}", tag=f"bank{c}") for c in range(CHUNKS)]
+
+        y_bank = [psum.tile([P, BANK], F32, name=f"y_bank{c}", tag=f"bank{c}") for c in range(CHUNKS)]
+        last_tile = PACK - 1
 
         def y_place(t, k):
-            if k >= 2 and t in (0, PACK - 1):
-                return y_bank[4 if k == 2 else 7][:, 256 * (t > 0):256 * (t > 0) + 256]
-            return y_bank[4 * (k // 2) + t][:, 256 * (k % 2):256 * (k % 2 + 1)]
+            if k >= 2 and t in (0, last_tile):
+                side = QUARTER * (t == last_tile)
+                return y_bank[PACK if k == 2 else PACK + last_tile][:, side:side + QUARTER]
+            return y_bank[PACK * (k // 2) + t][:, QUARTER * (k % 2):QUARTER * (k % 2 + 1)]
 
         def layer2(t, k):
-            cols = slice(256 * k, 256 * (k + 1))
+            cols = slice(QUARTER * k, QUARTER * (k + 1))
             nc.tensor.matmul_mx(
                 out=y_place(t, k),
                 lhsT=w2w[:, 2 * P * t:2 * P * (t + 1)].bitcast(FP4X4),
@@ -186,35 +202,39 @@ def tile_picked_zappnp_relu_po_kernel(
             nc.scalar.activation(dst, src, ACT.Copy, scale=scale)
 
         def empty_quarter(t, k):
-            scaled(y[t][:, 256 * k:256 * (k + 1)], y_place(t, k), KEEP)
+            scaled(y[t][:, QUARTER * k:QUARTER * (k + 1)], y_place(t, k), KEEP)
+
+        def empty_first_half(t):
+            scaled(y[t][:, 0:BANK], y_bank[t][:], KEEP)
 
         def empty_y(t):
-            scaled(y[t][:, 0:512], y_bank[t][:], KEEP)
-            if t == PACK - 1:
+            empty_first_half(t)
+            if t == last_tile:
                 empty_quarter(t, 2)
                 empty_quarter(t, 3)
-            elif t > 0:
-                scaled(y[t][:, 512:1024], y_bank[4 + t][:], KEEP)
+            else:
+                scaled(y[t][:, BANK:S], y_bank[PACK + t][:], KEEP)
 
         for k in range(3):
             for t in range(PACK):
                 layer2(t, k)
-        empty_y(0)
+        empty_first_half(0)
         empty_quarter(0, 2)
-        for t in range(PACK - 1):
+        for t in range(last_tile):
             layer2(t, 3)
-        nc.vector.tensor_scalar_mul(y[0][:, 768:1024], y_place(0, 3), KEEP)
-        layer2(PACK - 1, 3)
+        nc.vector.tensor_scalar_mul(y[0][:, 3 * QUARTER:S], y_place(0, 3), KEEP)
+        layer2(last_tile, 3)
 
-        def own(window, lst, n, scale, name):
-            c = held.tile([P, n], F32, name=name)
-            nc.scalar.activation(c[:], window[:].indirect(lst[:]), ACT.Copy, scale=scale)
-            return c
 
-        def near(window, lst, weights, n, name):
-            a = held.tile([P, n], F32, name=name)
-            nc.vector.tensor_tensor(a[:], window[:].indirect(lst[:]), weights, ALU.mult)
-            return a
+        def fetch(window, lst, n, scale, name):
+            term = held.tile([P, n], F32, name=name)
+            nc.scalar.activation(term[:], window[:].indirect(lst[:]), ACT.Copy, scale=scale)
+            return term
+
+        def fetch_gated(window, lst, weights, n, name):
+            term = held.tile([P, n], F32, name=name)
+            nc.vector.tensor_tensor(term[:], window[:].indirect(lst[:]), weights, ALU.mult)
+            return term
 
         def turn(bank, term, first, last):
             blocks = term.shape[1] // P
@@ -223,92 +243,95 @@ def tile_picked_zappnp_relu_po_kernel(
                 nc.tensor.matmul(bank[:, cols], lhsT=term[:, cols], rhs=ident[:], is_transpose=True,
                                  start=(first and blk == 0), stop=(last and blk == blocks - 1))
 
-        sum_bank, back_bank, z_turned, own2 = {}, {}, {}, {}
+        z_sum, z_back = {}, {}
 
-        def mix1_gathers(t):
-            c1 = own(y[t], cen_t, V, KEEP / MIX, f"own1_{t}")
-            a1 = near(y[t], pos1_t, gate_t[:, 0, :], V, f"a1_{t}")
-            b1 = near(y[t], pos2_t, gate_t[:, 1, :], V, f"b1_{t}")
-            sum_bank[t] = psum.tile([P, V], F32, name=f"sum_bank{t}", tag=f"bank{t}")
-            turn(sum_bank[t], a1, True, False)
-            turn(sum_bank[t], c1, False, False)
-            turn(sum_bank[t], b1, False, True)
+        def mix1_sum(t):
+            own = fetch(y[t], cen_t, V, KEEP / MIX, f"own1_{t}")
+            near_a = fetch_gated(y[t], pos1_t, gate_t[:, 0, :], V, f"a1_{t}")
+            near_b = fetch_gated(y[t], pos2_t, gate_t[:, 1, :], V, f"b1_{t}")
+            z_sum[t] = psum.tile([P, V], F32, name=f"z_sum{t}", tag=f"bank{t}")
+            turn(z_sum[t], near_a, True, False)
+            turn(z_sum[t], own, False, False)
+            turn(z_sum[t], near_b, False, True)
 
-        def mix1_scale(t):
-            z_turned[t] = held.tile([P, V], F32, name=f"z_turned{t}")
-            scaled(z_turned[t][:], sum_bank[t][:], MIX * MIX / KEEP)
-            back_bank[t] = psum.tile([P, V], F32, name=f"back_bank{t}", tag=f"bank{4 + t}")
-            turn(back_bank[t], z_turned[t], True, True)
+        def mix1_turn_back(t):
+            turned = held.tile([P, V], F32, name=f"z_turned{t}")
+            scaled(turned[:], z_sum[t][:], MIX * MIX / KEEP)
+            z_back[t] = psum.tile([P, V], F32, name=f"z_back{t}", tag=f"bank{PACK + t}")
+            turn(z_back[t], turned, True, True)
 
         def mix1_out(t):
-            nc.scalar.copy(out=z[t][:], in_=back_bank[t][:])
+            nc.scalar.copy(out=z[t][:], in_=z_back[t][:])
 
-        def mix2_own(t):
-            own2[t] = own(y[t], root_t, U, 1.0, f"own2_{t}")
+        def mix2_a(t):
+            return fetch_gated(z[t], nxt1_t, gate2_t[:, 0, :], U, f"a2_{t}")
 
-        def mix2_near(t):
-            return (near(z[t], nxt1_t, gate2_t[:, 0, :], U, f"a2_{t}"),
-                    near(z[t], nxt2_t, gate2_t[:, 1, :], U, f"b2_{t}"))
+        def mix2_b(t):
+            return fetch_gated(z[t], nxt2_t, gate2_t[:, 1, :], U, f"b2_{t}")
 
         def store(t):
             nc.sync.dma_start(out=out_rows[:, t, :], in_=res[:, t, :])
 
-        def mix2_turned(t, terms):
-            bank = psum.tile([P, U], F32, name=f"sum2_bank{t}", tag=f"bank{t}")
-            turn(bank, own2[t], True, False)
-            turn(bank, terms[0], False, False)
-            turn(bank, terms[1], False, True)
+        def mix2_turn(t, near_a, near_b, own):
+            bank = psum.tile([P, U], F32, name=f"res_sum{t}", tag=f"bank{t}")
+            turn(bank, near_a, True, False)
+            turn(bank, near_b, False, False)
+            turn(bank, own, False, True)
             turned = held.tile([P, U], F32, name=f"res_turned{t}")
             nc.scalar.copy(out=turned[:], in_=bank[:])
-            back = psum.tile([P, U], F32, name=f"back2_bank{t}", tag=f"bank{4 + t}")
+            back = psum.tile([P, U], F32, name=f"res_back{t}", tag=f"bank{PACK + t}")
             turn(back, turned, True, True)
-            nc.scalar.copy(out=res[:, t, :], in_=back[:])
-            store(t)
+            return back
 
-        def mix2_part(t, a):
-            s = held.tile([P, U], F32, name=f"s2_{t}")
-            nc.vector.tensor_tensor(s[:], y[t][:].indirect(root_t[:]), a[:], ALU.add)
-            return s
+        def mix2_add_root(t, near_a):
+            part = held.tile([P, U], F32, name=f"part2_{t}")
+            nc.vector.tensor_tensor(part[:], y[t][:].indirect(root_t[:]), near_a[:], ALU.add)
+            return part
 
-        def mix2_out(t, b, s):
-            nc.vector.tensor_tensor(res[:, t, :], b[:], s[:], ALU.add)
+        def mix2_add_rest(t, near_b, part):
+            nc.vector.tensor_tensor(res[:, t, :], near_b[:], part[:], ALU.add)
             store(t)
 
         for t in range(PACK):
             if t + 1 < PACK:
                 empty_y(t + 1)
             if t >= 2:
-                mix1_scale(t - 2)
-            mix1_gathers(t)
-            if t >= 2:
-                mix1_out(t - 2)
-        mix1_scale(2)
-        mix2_own(0)
-        terms0 = mix2_near(0)
+                mix1_turn_back(t - 2)
+            if t >= 3:
+                mix1_out(t - 3)
+            mix1_sum(t)
+        mix1_out(1)
+        mix1_turn_back(2)
+        mix1_turn_back(3)
+
+        near0 = (mix2_a(0), mix2_b(0))
         mix1_out(2)
-        mix1_scale(3)
-        mix2_own(1)
-        terms1 = mix2_near(1)
         mix1_out(3)
-        mix2_turned(0, terms0)
-        mix2_turned(1, terms1)
-        terms2 = mix2_near(2)
-        part2 = mix2_part(2, terms2[0])
-        a3 = near(z[3], nxt1_t, gate2_t[:, 0, :], U, "a2_3")
-        mix2_out(2, terms2[1], part2)
-        b3 = near(z[3], nxt2_t, gate2_t[:, 1, :], U, "b2_3")
-        part3 = mix2_part(3, a3)
-        mix2_out(3, b3, part3)
+        near1 = (mix2_a(1), mix2_b(1))
+        own2 = [fetch(y[t], root_t, U, 1.0, f"own2_{t}") for t in range(2)]
+        back = [mix2_turn(0, *near0, own2[0]), mix2_turn(1, *near1, own2[1])]
+        for t in range(2):
+            nc.scalar.copy(out=res[:, t, :], in_=back[t][:])
+            store(t)
+
+        near_a2, near_b2 = mix2_a(2), mix2_b(2)
+        part2 = mix2_add_root(2, near_a2)
+        near_a3 = mix2_a(3)
+        mix2_add_rest(2, near_b2, part2)
+        near_b3 = mix2_b(3)
+        mix2_add_rest(3, near_b3, mix2_add_root(3, near_a3))
+
 
         res_bf = held.tile([P, PACK * U], BF16, name="res_bf", align_bytes=64)
         res_codes = held.tile([P, U], U32, name="res_codes", align_bytes=64)
         res_scales = held.tile([P, U], U8, name="res_scales", align_bytes=64)
-        for copy, lo, hi in ((nc.scalar.copy, 0, 96), (nc.vector.tensor_copy, 96, U)):
-            copy(out=res_bf[:].rearrange("p (x t) -> p x t", t=PACK)[:, lo:hi],
-                 in_=res[:].rearrange("p t x -> p x t")[:, lo:hi])
+        woven = res_bf[:].rearrange("p (x t) -> p x t", t=PACK)
+        by_column = res[:].rearrange("p t x -> p x t")
+        nc.scalar.copy(out=woven[:, 0:OUT_SHARE], in_=by_column[:, 0:OUT_SHARE])
+        nc.vector.tensor_copy(out=woven[:, OUT_SHARE:U], in_=by_column[:, OUT_SHARE:U])
         nc.vector.quantize_mx(out=res_codes[:].bitcast(FP8X4), scales=res_scales[:], in_=res_bf[:])
         nc.sync.dma_start(out=out_1[0].rearrange("p n t -> p (n t)").bitcast(I32), in_=res_codes[:].bitcast(I32))
-        for q in range(4):
+        for q in range(QUADRANTS):
             queue = nc.scalar if q % 2 == 0 else nc.sync
             queue.dma_start(out=out_2[0, 4 * q:4 * q + 4, :].bitcast(I32),
                             in_=res_scales[32 * q:32 * q + 4, :].bitcast(I32))

from contextlib import ExitStack

import concourse.mybir as mybir
from concourse.masks import make_identity

K, T, S, V, H, N, U = 1024, 2048, 1024, 512, 512, 512, 256
FLOPS = 2 * K * H * S + 2 * H * N * S

F32 = mybir.dt.float32
BF16 = mybir.dt.bfloat16
I32 = mybir.dt.int32
U32 = mybir.dt.uint32
U16 = mybir.dt.uint16
U8 = mybir.dt.uint8
FP8X4 = mybir.dt.float8_e4m3fn_x4
FP4X4 = mybir.dt.float4_e2m1fn_x4
ACT = mybir.ActivationFunctionType
ALU = mybir.AluOpType

P = 128
PACK = 4
K_PASS = P * PACK
PASSES = K // K_PASS
QUADRANTS = 4
BANK = 512
CHUNK = BANK // PACK
CHUNKS = S // CHUNK
QUARTER = S // 4
LIST_ROWS = 16
MIX = 0.8
KEEP = 0.2

W1_SHARE = (96, 64)
OUT_SHARE = 96


def tile_picked_zappnp_relu_po_kernel(
    tc, x_words, x_scales, w1, w2_words, w2_scales, gate, gate2,
    offs, cen, pos1, pos2, nxt1, nxt2, root, out_0, out_1, out_2,
):
    nc = tc.nc
    with ExitStack() as ctx:
        held = ctx.enter_context(tc.tile_pool(name="held", bufs=1))
        psum = ctx.enter_context(tc.psum_pool(name="psum", bufs=1))


        def load_list(name, entries):
            lst = held.tile(list(entries.shape), U16, name=name)
            nc.sync.dma_start(lst[:], entries)
            return lst

        def load_w1(o):
            raw = held.tile([P, PACK, H], F32, name=f"w1_raw{o}")
            rows = w1[o * K_PASS:(o + 1) * K_PASS, :]
            nc.sync.dma_start(out=raw[:], in_=rows.rearrange("(p j) c -> p j c", j=PACK))
            return raw

        def load_x(o):
            table = held.tile([P, T], I32, name=f"x_table{o}")
            nc.sync.dma_start(out=table[:], in_=x_words[o].rearrange("p n t -> p (n t)").bitcast(I32))
            return table

        xs_table = held.tile([P, T], U8, name="xs_table", align_bytes=64)
        nc.vector.memset(xs_table[:].bitcast(I32), 0)
        w2s_raw = held.tile([P, N], U8, name="w2s_raw", align_bytes=64)
        nc.gpsimd.memset(w2s_raw[:].bitcast(I32), 0)

        offs_t = load_list("offs_t", offs)
        w1_raw = [load_w1(0)]
        for q in range(QUADRANTS):
            nc.sync.dma_start(out=xs_table[32 * q:32 * q + 4 * PASSES, :].bitcast(I32),
                              in_=x_scales[:, 4 * q:4 * q + 4, :].bitcast(I32))
        x_table = [load_x(0)]
        for q in range(QUADRANTS):
            nc.gpsimd.dma_start(out=w2s_raw[32 * q:32 * q + 4, :].bitcast(I32),
                                in_=w2_scales[0, 4 * q:4 * q + 4, :].bitcast(I32))
        w1_raw.append(load_w1(1))
        x_table.append(load_x(1))
        w2w_raw = held.tile([P, 2 * N], U8, name="w2w_raw", align_bytes=64)
        nc.sync.dma_start(out=w2w_raw[:].bitcast(I32), in_=w2_words[0].bitcast(I32))
        pos1_t = load_list("pos1_t", pos1)
        pos2_t = load_list("pos2_t", pos2)
        cen_t = load_list("cen_t", cen)
        gate_t = held.tile([P, 2, V], F32, name="gate_t")
        nc.sync.dma_start(out=gate_t[:], in_=gate.rearrange("d p v -> p d v"))
        nxt1_t = load_list("nxt1_t", nxt1)
        nxt2_t = load_list("nxt2_t", nxt2)
        root_t = load_list("root_t", root)
        gate2_t = held.tile([P, 2, U], F32, name="gate2_t")
        nc.sync.dma_start(out=gate2_t[:], in_=gate2.rearrange("d p v -> p d v"))

        w2s = held.tile([P, N], U8, name="w2s", align_bytes=64)
        nc.gpsimd.tensor_copy(out=w2s[:].rearrange("p (t m) -> p t m", t=PACK),
                              in_=w2s_raw[:].rearrange("p (m t) -> p t m", t=PACK))

        ident = held.tile([P, P], F32, name="ident")
        make_identity(nc, ident[:])


        w1_bf = [held.tile([P, PACK * H], BF16, name=f"w1_bf{o}", align_bytes=64) for o in range(PASSES)]
        w1_codes = [held.tile([P, H], U32, name=f"w1_codes{o}", align_bytes=64) for o in range(PASSES)]
        w1_scales = [held.tile([P, H], U8, name=f"w1_scales{o}", align_bytes=64) for o in range(PASSES)]
        x_codes = [held.tile([P, S], U32, name=f"x_codes{o}", align_bytes=64) for o in range(PASSES)]
        x_sc = held.tile([P, S], U8, name="x_sc", align_bytes=64)

        def round_w1(o):
            dst = w1_bf[o][:].rearrange("p (t m j) -> p m t j", t=PACK, j=PACK)
            src = w1_raw[o][:].rearrange("p j (m t) -> p m t j", t=PACK)
            share = W1_SHARE[o]
            nc.scalar.copy(out=dst[:, 0:share], in_=src[:, 0:share])
            nc.vector.tensor_copy(out=dst[:, share:P], in_=src[:, share:P])

        def quantize_w1(o):
            nc.vector.quantize_mx(out=w1_codes[o][:].bitcast(FP8X4), scales=w1_scales[o][:], in_=w1_bf[o][:])

        def gather_x(o, lo, hi):
            entries = offs_t[:, lo // LIST_ROWS:hi // LIST_ROWS]
            nc.vector.tensor_copy(x_codes[o][:, lo:hi], x_table[o][:].bitcast(U32).indirect(entries))

        h_bank = [psum.tile([P, PACK, CHUNK], F32, name=f"h_bank{c}", tag=f"bank{c}") for c in range(CHUNKS)]

        def layer1(o, c):
            cols = slice(c * CHUNK, (c + 1) * CHUNK)
            for t in range(PACK):
                nc.tensor.matmul_mx(
                    out=h_bank[c][:, t, :],
                    lhsT=w1_codes[o][:, t * P:(t + 1) * P].bitcast(FP8X4),
                    lhsT_scale=w1_scales[o][:, t * P:(t + 1) * P],
                    rhs=x_codes[o][:, cols].bitcast(FP8X4),
                    rhs_scale=x_sc[4 * o:P, cols],
                    start=(o == 0 and t == 0),
                    stop=(o == PASSES - 1 and t == PACK - 1),
                )

        round_w1(0)
        nc.vector.tensor_copy(x_sc[:], xs_table[:].indirect(offs_t[:]))
        quantize_w1(0)
        for lo, hi in ((0, QUARTER), (QUARTER, 2 * QUARTER), (2 * QUARTER, S)):
            gather_x(0, lo, hi)
        for c in range(CHUNKS):
            layer1(0, c)
        round_w1(1)
        quantize_w1(1)

        w2w = held.tile([P, 2 * N], U8, name="w2w", align_bytes=64)
        nc.scalar.copy(out=w2w[:].bitcast(U16).rearrange("p (t m) -> p t m", t=PACK),
                       in_=w2w_raw[:].bitcast(U16).rearrange("p (m t) -> p t m", t=PACK))

        h_bf = held.tile([P, PACK * S], BF16, name="h_bf", align_bytes=64)
        h_codes = held.tile([P, S], U32, name="h_codes", align_bytes=64)
        h_scales = held.tile([P, S], U8, name="h_scales", align_bytes=64)

        def relu(c, on_vector):
            dst = h_bf[:, c * BANK:(c + 1) * BANK].rearrange("p (n t) -> p n t", t=PACK)
            src = h_bank[c][:].rearrange("p t n -> p n t")
            if on_vector:
                nc.vector.tensor_scalar_max(dst, src, 0.0)
            else:
                nc.scalar.activation(dst, src, ACT.Relu)

        def quantize_h(k):
            cols = slice(QUARTER * k, QUARTER * (k + 1))
            nc.vector.quantize_mx(out=h_codes[:, cols].bitcast(FP8X4), scales=h_scales[:, cols],
                                  in_=h_bf[:, PACK * QUARTER * k:PACK * QUARTER * (k + 1)])

        for k in range(4):
            gather_x(1, QUARTER * k, QUARTER * (k + 1))
            layer1(1, 2 * k)
            layer1(1, 2 * k + 1)
        for k in range(4):
            relu(2 * k, on_vector=k >= 2)
            relu(2 * k + 1, on_vector=False)
            quantize_h(k)


        y_bank = [psum.tile([P, BANK], F32, name=f"y_bank{c}", tag=f"bank{c}") for c in range(CHUNKS)]
        last_tile = PACK - 1

        def y_place(t, k):
            if k >= 2 and t in (0, last_tile):
                side = QUARTER * (t == last_tile)
                return y_bank[PACK if k == 2 else PACK + last_tile][:, side:side + QUARTER]
            return y_bank[PACK * (k // 2) + t][:, QUARTER * (k % 2):QUARTER * (k % 2 + 1)]

        def layer2(t, k):
            cols = slice(QUARTER * k, QUARTER * (k + 1))
            nc.tensor.matmul_mx(
                out=y_place(t, k),
                lhsT=w2w[:, 2 * P * t:2 * P * (t + 1)].bitcast(FP4X4),
                lhsT_scale=w2s[:, P * t:P * (t + 1)],
                rhs=h_codes[:, cols].bitcast(FP8X4),
                rhs_scale=h_scales[:, cols],
                start=True, stop=True,
            )

        y = [held.tile([P, S], F32, name=f"y{t}") for t in range(PACK)]
        z = [held.tile([P, V], F32, name=f"z{t}") for t in range(PACK)]
        res = held.tile([P, PACK, U], F32, name="res")
        out_rows = out_0.rearrange("(p t) x -> p t x", t=PACK)

        def scaled(dst, src, scale):
            nc.scalar.activation(dst, src, ACT.Copy, scale=scale)

        def empty_quarter(t, k):
            scaled(y[t][:, QUARTER * k:QUARTER * (k + 1)], y_place(t, k), KEEP)

        def empty_first_half(t):
            scaled(y[t][:, 0:BANK], y_bank[t][:], KEEP)

        def empty_y(t):
            empty_first_half(t)
            if t == last_tile:
                empty_quarter(t, 2)
                empty_quarter(t, 3)
            else:
                scaled(y[t][:, BANK:S], y_bank[PACK + t][:], KEEP)

        for k in range(3):
            for t in range(PACK):
                layer2(t, k)
        empty_first_half(0)
        empty_quarter(0, 2)
        for t in range(last_tile):
            layer2(t, 3)
        nc.vector.tensor_scalar_mul(y[0][:, 3 * QUARTER:S], y_place(0, 3), KEEP)
        layer2(last_tile, 3)


        def fetch(window, lst, n, scale, name):
            term = held.tile([P, n], F32, name=name)
            nc.scalar.activation(term[:], window[:].indirect(lst[:]), ACT.Copy, scale=scale)
            return term

        def fetch_gated(window, lst, weights, n, name):
            term = held.tile([P, n], F32, name=name)
            nc.vector.tensor_tensor(term[:], window[:].indirect(lst[:]), weights, ALU.mult)
            return term

        def turn(bank, term, first, last):
            blocks = term.shape[1] // P
            for blk in range(blocks):
                cols = slice(blk * P, (blk + 1) * P)
                nc.tensor.matmul(bank[:, cols], lhsT=term[:, cols], rhs=ident[:], is_transpose=True,
                                 start=(first and blk == 0), stop=(last and blk == blocks - 1))

        z_sum, z_back = {}, {}

        def mix1_sum(t):
            own = fetch(y[t], cen_t, V, KEEP / MIX, f"own1_{t}")
            near_a = fetch_gated(y[t], pos1_t, gate_t[:, 0, :], V, f"a1_{t}")
            near_b = fetch_gated(y[t], pos2_t, gate_t[:, 1, :], V, f"b1_{t}")
            z_sum[t] = psum.tile([P, V], F32, name=f"z_sum{t}", tag=f"bank{t}")
            turn(z_sum[t], near_a, True, False)
            turn(z_sum[t], own, False, False)
            turn(z_sum[t], near_b, False, True)

        def mix1_turn_back(t):
            turned = held.tile([P, V], F32, name=f"z_turned{t}")
            scaled(turned[:], z_sum[t][:], MIX * MIX / KEEP)
            z_back[t] = psum.tile([P, V], F32, name=f"z_back{t}", tag=f"bank{PACK + t}")
            turn(z_back[t], turned, True, True)

        def mix1_out(t):
            nc.scalar.copy(out=z[t][:], in_=z_back[t][:])

        def mix2_a(t):
            return fetch_gated(z[t], nxt1_t, gate2_t[:, 0, :], U, f"a2_{t}")

        def mix2_b(t):
            return fetch_gated(z[t], nxt2_t, gate2_t[:, 1, :], U, f"b2_{t}")

        def store(t):
            nc.sync.dma_start(out=out_rows[:, t, :], in_=res[:, t, :])

        def mix2_turn(t, near_a, near_b, own):
            bank = psum.tile([P, U], F32, name=f"res_sum{t}", tag=f"bank{t}")
            turn(bank, near_a, True, False)
            turn(bank, near_b, False, False)
            turn(bank, own, False, True)
            turned = held.tile([P, U], F32, name=f"res_turned{t}")
            nc.scalar.copy(out=turned[:], in_=bank[:])
            back = psum.tile([P, U], F32, name=f"res_back{t}", tag=f"bank{PACK + t}")
            turn(back, turned, True, True)
            return back

        def mix2_add_root(t, near_a):
            part = held.tile([P, U], F32, name=f"part2_{t}")
            nc.vector.tensor_tensor(part[:], y[t][:].indirect(root_t[:]), near_a[:], ALU.add)
            return part

        def mix2_add_rest(t, near_b, part):
            nc.vector.tensor_tensor(res[:, t, :], near_b[:], part[:], ALU.add)
            store(t)

        for t in range(PACK):
            if t + 1 < PACK:
                empty_y(t + 1)
            if t >= 2:
                mix1_turn_back(t - 2)
            if t >= 3:
                mix1_out(t - 3)
            mix1_sum(t)
        mix1_out(1)
        mix1_turn_back(2)
        mix1_turn_back(3)

        near0 = (mix2_a(0), mix2_b(0))
        mix1_out(2)
        mix1_out(3)
        near1 = (mix2_a(1), mix2_b(1))
        own2 = [fetch(y[t], root_t, U, 1.0, f"own2_{t}") for t in range(2)]
        back = [mix2_turn(0, *near0, own2[0]), mix2_turn(1, *near1, own2[1])]
        for t in range(2):
            nc.scalar.copy(out=res[:, t, :], in_=back[t][:])
            store(t)

        near_a2, near_b2 = mix2_a(2), mix2_b(2)
        part2 = mix2_add_root(2, near_a2)
        near_a3 = mix2_a(3)
        mix2_add_rest(2, near_b2, part2)
        near_b3 = mix2_b(3)
        mix2_add_rest(3, near_b3, mix2_add_root(3, near_a3))


        res_bf = held.tile([P, PACK * U], BF16, name="res_bf", align_bytes=64)
        res_codes = held.tile([P, U], U32, name="res_codes", align_bytes=64)
        res_scales = held.tile([P, U], U8, name="res_scales", align_bytes=64)
        woven = res_bf[:].rearrange("p (x t) -> p x t", t=PACK)
        by_column = res[:].rearrange("p t x -> p x t")
        nc.scalar.copy(out=woven[:, 0:OUT_SHARE], in_=by_column[:, 0:OUT_SHARE])
        nc.vector.tensor_copy(out=woven[:, OUT_SHARE:U], in_=by_column[:, OUT_SHARE:U])
        nc.vector.quantize_mx(out=res_codes[:].bitcast(FP8X4), scales=res_scales[:], in_=res_bf[:])
        nc.sync.dma_start(out=out_1[0].rearrange("p n t -> p (n t)").bitcast(I32), in_=res_codes[:].bitcast(I32))
        for q in range(QUADRANTS):
            queue = nc.scalar if q % 2 == 0 else nc.sync
            queue.dma_start(out=out_2[0, 4 * q:4 * q + 4, :].bitcast(I32),
                            in_=res_scales[32 * q:32 * q + 4, :].bitcast(I32))
